import numpy as np, ml_dtypes
CORES = [5,13,29,37,53,69,77,101,133,141,157,165,181,197,205,229]
N = 16
NB, B = 6, 64
def setup_inputs(rng):
    return {"x": rng.standard_normal((N, 128, NB * B), dtype=np.float32).astype(ml_dtypes.bfloat16), "wv": (rng.standard_normal((N, 128, 128), dtype=np.float32) / 16).astype(ml_dtypes.bfloat16), "wh": (rng.standard_normal((N, 128, 128), dtype=np.float32) / 16).astype(ml_dtypes.bfloat16)}
def setup_inputs_big(rng):
    d = setup_inputs(rng)
    for k in ("x",): d[k] = (d[k].astype(np.float32) * 1048576.0).astype(d[k].dtype)
    return d
def setup_inputs_small(rng):
    d = setup_inputs(rng)
    for k in ("x",): d[k] = (d[k].astype(np.float32) * (1 / 1048576.0)).astype(d[k].dtype)
    return d
def setup_inputs_apart(rng):
    d = setup_inputs(rng)
    f = (10.0 ** rng.permutation(np.linspace(-1.5, 1.5, N))).astype(np.float32).reshape(N, 1, 1)
    for k in ("x",): d[k] = (d[k].astype(np.float32) * f).astype(d[k].dtype)
    return d
def reference(x, wv, wh):
    X, WV, WH = x.astype(np.float64), wv.astype(np.float64), wh.astype(np.float64)
    h = np.zeros((N, NB, 128, B))
    for r in range(N):
        for c in range(NB):
            a = X[r][:, B * c:B * c + B].copy()
            if r: a += WV[r].T @ h[r - 1][c]
            if c: a += WH[r].T @ h[r][c - 1]
            h[r][c] = np.maximum(a, 0.0)
    return {"y": np.concatenate([h[:, c] for c in range(NB)], axis=2).astype(ml_dtypes.bfloat16)}

@@ -1,0 +1,258 @@
+from concourse.mybir import AluOpType
+
+NB, B = 6, 64
+XW = NB * B
+WW = 128
+SLOT = XW + 2 * WW
+GROUPS = [(0, 1, 0), (1, 3, 1), (3, 10, 3), (10, 15, 11), (15, 16, 15)]
+KMAX = max(b - a for a, b, _ in GROUPS)
+NBANK = 8
+ENG = 8
+
+SCRATCH = {
+    "gin": ("sbuf", [128, KMAX * SLOT], "bfloat16"),
+    "hin": ("sbuf", [128, XW], "bfloat16"),
+    "hout": ("sbuf", [128, KMAX * XW], "bfloat16"),
+    "yl": ("sbuf", [128, XW], "bfloat16"),
+    "idz": ("sbuf", [128, 129], "bfloat16"),
+    "idd": ("dram", [129, 128], "bfloat16"),
+    "ident": ("sbuf", [128, 128], "bfloat16"),
+    "z32": ("sbuf", [128, B], "float32"),
+    "z16": ("sbuf", [128, B], "bfloat16"),
+}
+for _i in range(NBANK):
+    SCRATCH["ps%d" % _i] = ("psum", [128, 512], "float32")
+
+SEMAPHORES = (["ld", "rs", "st", "ls", "md", "vd", "va", "zs", "iz", "id1", "id2", "lx0", "lx1", "lw", "ys"]
+              + ["gs%d" % j for j in range(KMAX)] + ["fw%d" % c for c in range(NB)])
+
+
+def _plan(T, topo):
+    cores = list(T.cores)
+    hosts = max(topo.host(c) for c in cores) + 1
+    world = range(hosts * topo.CORES_PER_HOST)
+    used = set(cores)
+
+    def helper(near, srcs, dsts):
+        cand = [q for q in world
+                if q not in used and topo.host(q) == topo.host(near) and topo.chip(q) == topo.chip(near)
+                and all(topo.may_write(s, q) for s in srcs) and all(topo.may_write(q, d) for d in dsts)]
+        cand.sort(key=lambda q: (topo.die(q) != topo.die(near), q))
+        used.add(cand[0])
+        return cand[0]
+
+    n = len(GROUPS)
+    sites, frelay, grelay = [None] * n, [None] * n, {}
+    for gi in reversed(range(n)):
+        a, b, anchor = GROUPS[gi]
+        nxt = [sites[gi + 1]] if gi + 1 < n else []
+        if b - a == 1:
+            sites[gi] = cores[a]
+            if nxt and not topo.may_write(cores[a], nxt[0]):
+                frelay[gi] = helper(cores[a], [cores[a]], nxt)
+        else:
+            sites[gi] = helper(cores[anchor], [], [cores[r] for r in range(a, b)] + nxt)
+            for r in range(a, b):
+                if not topo.may_write(cores[r], sites[gi]):
+                    grelay[r] = helper(cores[r], [cores[r]], [sites[gi]])
+    return sites, frelay, grelay
+
+
+def _engines(topo, src, dst, n, high):
+    m = topo.mask(src, dst)
+    bits = [e for e in range(m.bit_length()) if (m >> e) & 1]
+    return sum(1 << e for e in (bits[-n:] if high else bits[:n]))
+
+
+def rank_program(g, core, T, topo):
+    sites, frelay, grelay = _plan(T, topo)
+    cores = list(T.cores)
+    S = T.sem
+    sent = [0]
+
+    def waiter(q):
+        seen = {}
+
+        def w(name, val):
+            if seen.get(name, 0) < val:
+                q.wait_ge(S[name], val)
+                seen[name] = val
+        return w
+
+    gw, tw, vw, sw, cw = waiter(g), waiter(g.tensor), waiter(g.vector), waiter(g.sync), waiter(g.scalar)
+
+    def send(dst, out_ap, in_ap, rsem, high=False):
+        rid, pid = topo.addr(dst, core)
+        g.remote_dma(out_ap=out_ap, in_ap=in_ap, remote_sem=S[rsem], local_sem=S.ls, pid=pid, routing_id=rid,
+                     dma_engine_mask=_engines(topo, core, dst, ENG, high))
+        sent[0] += ENG
+
+    def col(c0, c1=None):
+        return slice(c0 * B, (c0 + 1 if c1 is None else c1) * B)
+
+    for r, q in grelay.items():
+        if q == core:
+            gi = [i for i, (a, b, _) in enumerate(GROUPS) if a <= r < b][0]
+            j = r - GROUPS[gi][0]
+            gw("rs", ENG)
+            send(sites[gi], T.gin[:, j * SLOT:(j + 1) * SLOT], T.gin[:, 0:SLOT], "gs%d" % j)
+            gw("ls", sent[0])
+            return
+
+    for gi, q in enumerate(frelay):
+        if q == core:
+            for c in range(NB):
+                gw("fw%d" % c, ENG)
+                send(sites[gi + 1], T.hin[:, col(c)], T.hin[:, col(c)], "fw%d" % c)
+            gw("ls", sent[0])
+            return
+
+    rank = T.rank_of(core)
+    if core not in sites:
+        if rank is None:
+            return
+        gi = [i for i, (a, b, _) in enumerate(GROUPS) if a <= rank < b][0]
+        j = rank - GROUPS[gi][0]
+        g.sync.dma_start(T.gin[:, 0:XW], T.x[:]).then_inc(S.ld, 16)
+        g.scalar.dma_start(T.gin[:, XW:XW + WW], T.wv[:]).then_inc(S.ld, 16)
+        g.scalar.dma_start(T.gin[:, XW + WW:SLOT], T.wh[:]).then_inc(S.ld, 16)
+        gw("ld", 48)
+        if rank in grelay:
+            send(grelay[rank], T.gin[:, 0:SLOT], T.gin[:, 0:SLOT], "rs")
+        else:
+            send(sites[gi], T.gin[:, j * SLOT:(j + 1) * SLOT], T.gin[:, 0:SLOT], "gs%d" % j)
+        sw("ys", ENG)
+        g.sync.dma_start(T.y[:], T.yl[:]).then_inc(S.st, 16)
+        gw("ls", sent[0])
+        gw("st", 16)
+        return
+
+    gi = sites.index(core)
+    a, b, _ = GROUPS[gi]
+    k = b - a
+    own = rank is not None
+    first = a == 0
+    fdst = None
+    if gi + 1 < len(GROUPS):
+        fdst = frelay[gi] if frelay[gi] is not None else sites[gi + 1]
+
+    def hap(j, c):
+        return T.hout[:, j * XW + c * B:j * XW + (c + 1) * B]
+
+    def xap(j, c):
+        return T.gin[:, j * SLOT + c * B:j * SLOT + (c + 1) * B]
+
+    def wvap(j):
+        return T.gin[:, j * SLOT + XW:j * SLOT + XW + WW]
+
+    def whap(j):
+        return T.gin[:, j * SLOT + XW + WW:(j + 1) * SLOT]
+
+    g.vector.memset(T.z32[:], 0.0).then_inc(S.zs, 1)
+    nz = 1
+    if first:
+        g.vector.memset(T.z16[:], 0.0).then_inc(S.zs, 1)
+        nz = 2
+        g.sync.dma_start(xap(0, 0), T.x[:, col(0)]).then_inc(S.lx0, 16)
+        g.scalar.dma_start(whap(0), T.wh[:]).then_inc(S.lw, 16)
+        g.sync.dma_start(T.gin[:, B:XW], T.x[:, B:XW]).then_inc(S.lx1, 16)
+    else:
+        g.vector.memset(T.idz[:], 0.0).then_inc(S.iz, 1)
+        vw("iz", 1)
+        g.vector.memset(T.idz[:, 0:1], 1.0).then_inc(S.iz, 1)
+        sw("iz", 2)
+        g.sync.dma_start(T.idd[:], T.idz[:]).then_inc(S.id1, 16)
+        sw("id1", 16)
+        g.sync.dma_start(T.ident[:], T.idd[0:128, :]).then_inc(S.id2, 16)
+        if own:
+            g.scalar.dma_start(T.gin[:, 0:XW], T.x[:]).then_inc(S.gs0, 16)
+            g.scalar.dma_start(wvap(0), T.wv[:]).then_inc(S.gs0, 16)
+            g.scalar.dma_start(whap(0), T.wh[:]).then_inc(S.gs0, 16)
+    vw("zs", nz)
+
+    def got(w, j, what, c=0):
+        if first:
+            if what == "w":
+                w("lw", 16)
+            else:
+                w("lx0" if c == 0 else "lx1", 16)
+        else:
+            w("gs%d" % j, 48 if own else ENG)
+
+    def mats(i):
+        c, j = divmod(i, k)
+        m = []
+        if not first:
+            m.append((T.ident[:], xap(j, c), -1, -1, j))
+        if c > 0:
+            m.append((whap(j), hap(j, c - 1), i - k, -1, j))
+        if a + j > 0:
+            if j > 0:
+                m.append((wvap(j), hap(j - 1, c), i - 1, -1, j))
+            else:
+                m.append((wvap(j), T.hin[:, col(c)], -1, c, j))
+        return m
+
+    def is_early(i, e):
+        return e[2] <= i - 2 and e[3] < 0
+
+    def issue(i, early):
+        m = mats(i)
+        ps = T["ps%d" % (i % NBANK)][:, 0:B]
+        for n_, e in enumerate(m):
+            if is_early(i, e) != early:
+                continue
+            if not first and n_ == 0:
+                tw("id2", 16)
+            got(tw, e[4], "w")
+            if e[3] >= 0:
+                tw("fw%d" % e[3], ENG)
+            ins = g.tensor.matmul(ps, e[0], e[1], n_ == 0, n_ == len(m) - 1)
+            if n_ == len(m) - 1:
+                ins.then_inc(S.md, 1)
+
+    nblk = NB * k
+    nmd, nva = 0, 0
+    issue(0, True)
+    for i in range(nblk):
+        c, j = divmod(i, k)
+        ps = T["ps%d" % (i % NBANK)][:, 0:B]
+        tw("vd", i)
+        issue(i, False)
+        if i + 1 < nblk:
+            issue(i + 1, True)
+        if mats(i):
+            nmd += 1
+            vw("md", nmd)
+            if first:
+                got(vw, j, "x", c)
+                g.vector.tensor_tensor(ps, ps, xap(j, c), AluOpType.add).then_inc(S.va, 1)
+                nva += 1
+                vw("va", nva)
+            g.vector.tensor_tensor(hap(j, c), ps, T.z32[:], AluOpType.max).then_inc(S.vd, 1)
+        else:
+            got(vw, j, "x", c)
+            g.vector.tensor_tensor(hap(j, c), xap(j, c), T.z16[:], AluOpType.max).then_inc(S.vd, 1)
+
+    nst = 0
+    for c in range(NB):
+        if fdst is not None:
+            gw("vd", k * (c + 1))
+            send(fdst, T.hin[:, col(c)], hap(k - 1, c), "fw%d" % c)
+        if own and not first:
+            q, w = (g.sync, sw) if c % 2 == 0 else (g.scalar, cw)
+            w("vd", c + 1)
+            q.dma_start(T.y[:, col(c)], hap(0, c)).then_inc(S.st, 16)
+            nst += 1
+    if own and first:
+        sw("vd", NB)
+        g.sync.dma_start(T.y[:], T.hout[:, 0:XW]).then_inc(S.st, 16)
+        nst += 1
+    if not own:
+        for j in range(k):
+            send(cores[a + j], T.yl[:], T.hout[:, j * XW:(j + 1) * XW], "ys", high=True)
+    gw("vd", nblk)
+    if sent[0]:
+        gw("ls", sent[0])
+    if nst:
+        gw("st", 16 * nst)

@@ -4,7 +4,7 @@ NB, B = 6, 64
 XW = NB * B
 WW = 128
 SLOT = XW + 2 * WW
-GROUPS = [(0, 1, 0), (1, 3, 1), (3, 10, 3), (10, 15, 11), (15, 16, 15)]
+GROUPS = [(0, 1, 0), (1, 3, 1), (3, 6, 3), (6, 10, 7), (10, 13, 11), (13, 15, 13), (15, 16, 15)]
 KMAX = max(b - a for a, b, _ in GROUPS)
 NBANK = 8
 ENG = 8

@@ -23,8 +23,9 @@ SCRATCH = {
 for _i in range(NBANK):
     SCRATCH["ps%d" % _i] = ("psum", [128, 512], "float32")
 
-SEMAPHORES = (["ld", "rs", "st", "ls", "md", "vd", "va", "zs", "iz", "id1", "id2", "lx0", "lx1", "lw", "ys"]
-              + ["gs%d" % j for j in range(KMAX)] + ["fw%d" % c for c in range(NB)])
+SEMAPHORES = (["ld", "rs", "st", "ls", "va", "zs", "iz", "id1", "id2", "lx0", "lx1", "lw", "ys"]
+              + ["gs%d" % j for j in range(KMAX)] + ["md%d" % j for j in range(KMAX)]
+              + ["vd%d" % j for j in range(KMAX)] + ["fw%d" % c for c in range(NB)])
 
 
 def _plan(T, topo):
@@ -179,79 +180,74 @@ def rank_program(g, core, T, topo):
         else:
             w("gs%d" % j, 48 if own else ENG)
 
-    def mats(i):
-        c, j = divmod(i, k)
+    seq = [(j, d - j) for d in range(NB + k - 1) for j in reversed(range(k)) if 0 <= d - j < NB]
+
+    def mats(j, c):
         m = []
         if not first:
-            m.append((T.ident[:], xap(j, c), -1, -1, j))
+            m.append((T.ident[:], xap(j, c), ("id2", 16)))
         if c > 0:
-            m.append((whap(j), hap(j, c - 1), i - k, -1, j))
+            m.append((whap(j), hap(j, c - 1), ("vd%d" % j, c)))
         if a + j > 0:
             if j > 0:
-                m.append((wvap(j), hap(j - 1, c), i - 1, -1, j))
+                m.append((wvap(j), hap(j - 1, c), ("vd%d" % (j - 1), c + 1)))
             else:
-                m.append((wvap(j), T.hin[:, col(c)], -1, c, j))
+                m.append((wvap(j), T.hin[:, col(c)], ("fw%d" % c, ENG)))
         return m
 
-    def is_early(i, e):
-        return e[2] <= i - 2 and e[3] < 0
-
-    def issue(i, early):
-        m = mats(i)
+    def issue(i, opening):
+        j, c = seq[i]
+        m = mats(j, c)
         ps = T["ps%d" % (i % NBANK)][:, 0:B]
         for n_, e in enumerate(m):
-            if is_early(i, e) != early:
+            if (not first and n_ == 0) != opening:
                 continue
-            if not first and n_ == 0:
-                tw("id2", 16)
-            got(tw, e[4], "w")
-            if e[3] >= 0:
-                tw("fw%d" % e[3], ENG)
+            if n_ == 0 and i >= NBANK:
+                pj, pc = seq[i - NBANK]
+                tw("vd%d" % pj, pc + 1)
+            got(tw, j, "w")
+            tw(e[2][0], e[2][1])
             ins = g.tensor.matmul(ps, e[0], e[1], n_ == 0, n_ == len(m) - 1)
             if n_ == len(m) - 1:
-                ins.then_inc(S.md, 1)
+                ins.then_inc(S["md%d" % j], 1)
 
-    nblk = NB * k
-    nmd, nva = 0, 0
+    nva = 0
     issue(0, True)
-    for i in range(nblk):
-        c, j = divmod(i, k)
+    for i, (j, c) in enumerate(seq):
         ps = T["ps%d" % (i % NBANK)][:, 0:B]
-        tw("vd", i)
-        issue(i, False)
-        if i + 1 < nblk:
+        if i + 1 < len(seq):
             issue(i + 1, True)
-        if mats(i):
-            nmd += 1
-            vw("md", nmd)
+        issue(i, False)
+        if mats(j, c):
+            vw("md%d" % j, c if first else c + 1)
             if first:
                 got(vw, j, "x", c)
                 g.vector.tensor_tensor(ps, ps, xap(j, c), AluOpType.add).then_inc(S.va, 1)
                 nva += 1
                 vw("va", nva)
-            g.vector.tensor_tensor(hap(j, c), ps, T.z32[:], AluOpType.max).then_inc(S.vd, 1)
+            g.vector.tensor_tensor(hap(j, c), ps, T.z32[:], AluOpType.max).then_inc(S["vd%d" % j], 1)
         else:
             got(vw, j, "x", c)
-            g.vector.tensor_tensor(hap(j, c), xap(j, c), T.z16[:], AluOpType.max).then_inc(S.vd, 1)
+            g.vector.tensor_tensor(hap(j, c), xap(j, c), T.z16[:], AluOpType.max).then_inc(S["vd%d" % j], 1)
 
     nst = 0
     for c in range(NB):
         if fdst is not None:
-            gw("vd", k * (c + 1))
+            gw("vd%d" % (k - 1), c + 1)
             send(fdst, T.hin[:, col(c)], hap(k - 1, c), "fw%d" % c)
         if own and not first:
             q, w = (g.sync, sw) if c % 2 == 0 else (g.scalar, cw)
-            w("vd", c + 1)
+            w("vd0", c + 1)
             q.dma_start(T.y[:, col(c)], hap(0, c)).then_inc(S.st, 16)
             nst += 1
     if own and first:
-        sw("vd", NB)
+        sw("vd0", NB)
         g.sync.dma_start(T.y[:], T.hout[:, 0:XW]).then_inc(S.st, 16)
         nst += 1
-    if not own:
-        for j in range(k):
+    for j in range(k):
+        gw("vd%d" % j, NB)
+        if not own:
             send(cores[a + j], T.yl[:], T.hout[:, j * XW:(j + 1) * XW], "ys", high=True)
-    gw("vd", nblk)
     if sent[0]:
         gw("ls", sent[0])
     if nst:

@@ -4,7 +4,9 @@ NB, B = 6, 64
 XW = NB * B
 WW = 128
 SLOT = XW + 2 * WW
-GROUPS = [(0, 1, 0), (1, 3, 1), (3, 6, 3), (6, 10, 7), (10, 13, 11), (13, 15, 13), (15, 16, 15)]
+GROUPS = [(0, 1, 0), (1, 3, 1), (3, 7, 3), (7, 11, 7), (11, 16, 15)]
+LAST_PIECES = [(0, 4), (4, NB)]
+OFFLOAD = 2
 KMAX = max(b - a for a, b, _ in GROUPS)
 NBANK = 8
 ENG = 8
@@ -23,7 +25,9 @@ SCRATCH = {
 for _i in range(NBANK):
     SCRATCH["ps%d" % _i] = ("psum", [128, 512], "float32")
 
-SEMAPHORES = (["ld", "rs", "st", "ls", "va", "zs", "iz", "id1", "id2", "lx0", "lx1", "lw", "ys"]
+SEMAPHORES = (["ld", "rs", "st", "ls", "va", "zs", "iz", "id1", "id2", "lx0", "lx1", "lw"]
+              + ["ys%d" % p for p in range(len(LAST_PIECES))]
+              + ["hs%d" % p for p in range(OFFLOAD * len(LAST_PIECES))]
               + ["gs%d" % j for j in range(KMAX)] + ["md%d" % j for j in range(KMAX)]
               + ["vd%d" % j for j in range(KMAX)] + ["fw%d" % c for c in range(NB)])
 
@@ -34,11 +38,11 @@ def _plan(T, topo):
     world = range(hosts * topo.CORES_PER_HOST)
     used = set(cores)
 
-    def helper(near, srcs, dsts):
+    def helper(near, srcs, dsts, same_die):
         cand = [q for q in world
                 if q not in used and topo.host(q) == topo.host(near) and topo.chip(q) == topo.chip(near)
                 and all(topo.may_write(s, q) for s in srcs) and all(topo.may_write(q, d) for d in dsts)]
-        cand.sort(key=lambda q: (topo.die(q) != topo.die(near), q))
+        cand.sort(key=lambda q: ((topo.die(q) == topo.die(near)) != same_die, q))
         used.add(cand[0])
         return cand[0]
 
@@ -50,13 +54,15 @@ def _plan(T, topo):
         if b - a == 1:
             sites[gi] = cores[a]
             if nxt and not topo.may_write(cores[a], nxt[0]):
-                frelay[gi] = helper(cores[a], [cores[a]], nxt)
+                frelay[gi] = helper(cores[a], [cores[a]], nxt, True)
         else:
-            sites[gi] = helper(cores[anchor], [], [cores[r] for r in range(a, b)] + nxt)
+            sites[gi] = helper(cores[anchor], [], [cores[r] for r in range(a, b)] + nxt, True)
             for r in range(a, b):
                 if not topo.may_write(cores[r], sites[gi]):
-                    grelay[r] = helper(cores[r], [cores[r]], [sites[gi]])
-    return sites, frelay, grelay
+                    grelay[r] = helper(cores[r], [cores[r]], [sites[gi]], False)
+    a = GROUPS[-1][0]
+    srelay = helper(sites[-1], [sites[-1]], cores[a:a + OFFLOAD], True)
+    return sites, frelay, grelay, srelay
 
 
 def _engines(topo, src, dst, n, high):
@@ -66,7 +72,7 @@ def _engines(topo, src, dst, n, high):
 
 
 def rank_program(g, core, T, topo):
-    sites, frelay, grelay = _plan(T, topo)
+    sites, frelay, grelay, srelay = _plan(T, topo)
     cores = list(T.cores)
     S = T.sem
     sent = [0]
@@ -91,6 +97,15 @@ def rank_program(g, core, T, topo):
     def col(c0, c1=None):
         return slice(c0 * B, (c0 + 1 if c1 is None else c1) * B)
 
+    def hap(j, c0, c1=None):
+        return T.hout[:, j * XW + c0 * B:j * XW + (c0 + 1 if c1 is None else c1) * B]
+
+    def pieces(gi):
+        return LAST_PIECES if gi == len(GROUPS) - 1 else [(0, NB)]
+
+    def todo(gi, k):
+        return [t[1:] for t in sorted((c1 + j, j, p, c0, c1) for j in range(k) for p, (c0, c1) in enumerate(pieces(gi)))]
+
     for r, q in grelay.items():
         if q == core:
             gi = [i for i, (a, b, _) in enumerate(GROUPS) if a <= r < b][0]
@@ -108,6 +123,13 @@ def rank_program(g, core, T, topo):
             gw("ls", sent[0])
             return
 
+    if core == srelay:
+        for j, p, c0, c1 in todo(len(GROUPS) - 1, OFFLOAD):
+            gw("hs%d" % (j * len(LAST_PIECES) + p), ENG)
+            send(cores[GROUPS[-1][0] + j], T.yl[:, col(c0, c1)], hap(j, c0, c1), "ys%d" % p)
+        gw("ls", sent[0])
+        return
+
     rank = T.rank_of(core)
     if core not in sites:
         if rank is None:
@@ -122,10 +144,11 @@ def rank_program(g, core, T, topo):
             send(grelay[rank], T.gin[:, 0:SLOT], T.gin[:, 0:SLOT], "rs")
         else:
             send(sites[gi], T.gin[:, j * SLOT:(j + 1) * SLOT], T.gin[:, 0:SLOT], "gs%d" % j)
-        sw("ys", ENG)
-        g.sync.dma_start(T.y[:], T.yl[:]).then_inc(S.st, 16)
+        for p, (c0, c1) in enumerate(pieces(gi)):
+            sw("ys%d" % p, ENG)
+            g.sync.dma_start(T.y[:, col(c0, c1)], T.yl[:, col(c0, c1)]).then_inc(S.st, 16)
         gw("ls", sent[0])
-        gw("st", 16)
+        gw("st", 16 * len(pieces(gi)))
         return
 
     gi = sites.index(core)
@@ -136,9 +159,6 @@ def rank_program(g, core, T, topo):
     fdst = None
     if gi + 1 < len(GROUPS):
         fdst = frelay[gi] if frelay[gi] is not None else sites[gi + 1]
-
-    def hap(j, c):
-        return T.hout[:, j * XW + c * B:j * XW + (c + 1) * B]
 
     def xap(j, c):
         return T.gin[:, j * SLOT + c * B:j * SLOT + (c + 1) * B]
@@ -244,10 +264,15 @@ def rank_program(g, core, T, topo):
         sw("vd0", NB)
         g.sync.dma_start(T.y[:], T.hout[:, 0:XW]).then_inc(S.st, 16)
         nst += 1
+    if not own:
+        for j, p, c0, c1 in todo(gi, k):
+            gw("vd%d" % j, c1)
+            if fdst is None and j < OFFLOAD:
+                send(srelay, hap(j, c0, c1), hap(j, c0, c1), "hs%d" % (j * len(LAST_PIECES) + p), high=True)
+            else:
+                send(cores[a + j], T.yl[:, col(c0, c1)], hap(j, c0, c1), "ys%d" % p, high=True)
     for j in range(k):
         gw("vd%d" % j, NB)
-        if not own:
-            send(cores[a + j], T.yl[:], T.hout[:, j * XW:(j + 1) * XW], "ys", high=True)
     if sent[0]:
         gw("ls", sent[0])
     if nst:

@@ -16,8 +16,7 @@ SCRATCH = {
     "hin": ("sbuf", [128, XW], "bfloat16"),
     "hout": ("sbuf", [128, KMAX * XW], "bfloat16"),
     "yl": ("sbuf", [128, XW], "bfloat16"),
-    "idz": ("sbuf", [128, 129], "bfloat16"),
-    "idd": ("dram", [129, 128], "bfloat16"),
+    "ones": ("sbuf", [128, 128], "bfloat16"),
     "ident": ("sbuf", [128, 128], "bfloat16"),
     "z32": ("sbuf", [128, B], "float32"),
     "z16": ("sbuf", [128, B], "bfloat16"),
@@ -25,7 +24,7 @@ SCRATCH = {
 for _i in range(NBANK):
     SCRATCH["ps%d" % _i] = ("psum", [128, 512], "float32")
 
-SEMAPHORES = (["ld", "rs", "st", "ls", "va", "zs", "iz", "id1", "id2", "lx0", "lx1", "lw"]
+SEMAPHORES = (["ld", "rs", "st", "ls", "va", "zs", "fil", "sel", "idn", "lx0", "lx1", "lw"]
               + ["ys%d" % p for p in range(len(LAST_PIECES))]
               + ["hs%d" % p for p in range(OFFLOAD * len(LAST_PIECES))]
               + ["gs%d" % j for j in range(KMAX)] + ["md%d" % j for j in range(KMAX)]
@@ -94,6 +93,13 @@ def rank_program(g, core, T, topo):
                      dma_engine_mask=_engines(topo, core, dst, ENG, high))
         sent[0] += ENG
 
+    def make_ident(dst):
+        g.vector.memset(T.ones[:], 1.0).then_inc(S.fil, 1)
+        gw("fil", 1)
+        g.affine_select(T.ident[:], T.ones[:], [[-1, 128]], AluOpType.is_equal, 0.0, 0, 1).then_inc(S.sel, 1)
+        gw("sel", 1)
+        send(dst, T.ident[:], T.ident[:], "idn")
+
     def col(c0, c1=None):
         return slice(c0 * B, (c0 + 1 if c1 is None else c1) * B)
 
@@ -117,6 +123,8 @@ def rank_program(g, core, T, topo):
 
     for gi, q in enumerate(frelay):
         if q == core:
+            if gi == 0:
+                make_ident(sites[gi + 1])
             for c in range(NB):
                 gw("fw%d" % c, ENG)
                 send(sites[gi + 1], T.hin[:, col(c)], T.hin[:, col(c)], "fw%d" % c)
@@ -177,14 +185,12 @@ def rank_program(g, core, T, topo):
         g.sync.dma_start(xap(0, 0), T.x[:, col(0)]).then_inc(S.lx0, 16)
         g.scalar.dma_start(whap(0), T.wh[:]).then_inc(S.lw, 16)
         g.sync.dma_start(T.gin[:, B:XW], T.x[:, B:XW]).then_inc(S.lx1, 16)
+        if frelay[gi] is None and fdst is not None:
+            make_ident(fdst)
     else:
-        g.vector.memset(T.idz[:], 0.0).then_inc(S.iz, 1)
-        vw("iz", 1)
-        g.vector.memset(T.idz[:, 0:1], 1.0).then_inc(S.iz, 1)
-        sw("iz", 2)
-        g.sync.dma_start(T.idd[:], T.idz[:]).then_inc(S.id1, 16)
-        sw("id1", 16)
-        g.sync.dma_start(T.ident[:], T.idd[0:128, :]).then_inc(S.id2, 16)
+        if fdst is not None:
+            gw("idn", ENG)
+            send(fdst, T.ident[:], T.ident[:], "idn")
         if own:
             g.scalar.dma_start(T.gin[:, 0:XW], T.x[:]).then_inc(S.gs0, 16)
             g.scalar.dma_start(wvap(0), T.wv[:]).then_inc(S.gs0, 16)
@@ -205,7 +211,7 @@ def rank_program(g, core, T, topo):
     def mats(j, c):
         m = []
         if not first:
-            m.append((T.ident[:], xap(j, c), ("id2", 16)))
+            m.append((T.ident[:], xap(j, c), ("idn", ENG)))
         if c > 0:
             m.append((whap(j), hap(j, c - 1), ("vd%d" % j, c)))
         if a + j > 0:

from concourse.mybir import AluOpType

NB, B = 6, 64
XW = NB * B
WW = 128
SLOT = XW + 2 * WW
GROUPS = [(0, 1, 0), (1, 3, 1), (3, 7, 3), (7, 11, 7), (11, 16, 15)]
LAST_PIECES = [(0, 4), (4, NB)]
OFFLOAD = 2
KMAX = max(b - a for a, b, _ in GROUPS)
NBANK = 8
ENG = 8

SCRATCH = {
    "gin": ("sbuf", [128, KMAX * SLOT], "bfloat16"),
    "hin": ("sbuf", [128, XW], "bfloat16"),
    "hout": ("sbuf", [128, KMAX * XW], "bfloat16"),
    "yl": ("sbuf", [128, XW], "bfloat16"),
    "ones": ("sbuf", [128, 128], "bfloat16"),
    "ident": ("sbuf", [128, 128], "bfloat16"),
    "z32": ("sbuf", [128, B], "float32"),
    "z16": ("sbuf", [128, B], "bfloat16"),
}
for _i in range(NBANK):
    SCRATCH["ps%d" % _i] = ("psum", [128, 512], "float32")

SEMAPHORES = (["ld", "rs", "st", "ls", "va", "zs", "fil", "sel", "idn", "lx0", "lx1", "lw"]
              + ["ys%d" % p for p in range(len(LAST_PIECES))]
              + ["hs%d" % p for p in range(OFFLOAD * len(LAST_PIECES))]
              + ["gs%d" % j for j in range(KMAX)] + ["md%d" % j for j in range(KMAX)]
              + ["vd%d" % j for j in range(KMAX)] + ["fw%d" % c for c in range(NB)])


def _plan(T, topo):
    cores = list(T.cores)
    hosts = max(topo.host(c) for c in cores) + 1
    world = range(hosts * topo.CORES_PER_HOST)
    used = set(cores)

    def helper(near, srcs, dsts, same_die):
        cand = [q for q in world
                if q not in used and topo.host(q) == topo.host(near) and topo.chip(q) == topo.chip(near)
                and all(topo.may_write(s, q) for s in srcs) and all(topo.may_write(q, d) for d in dsts)]
        cand.sort(key=lambda q: ((topo.die(q) == topo.die(near)) != same_die, q))
        used.add(cand[0])
        return cand[0]

    n = len(GROUPS)
    sites, frelay, grelay = [None] * n, [None] * n, {}
    for gi in reversed(range(n)):
        a, b, anchor = GROUPS[gi]
        nxt = [sites[gi + 1]] if gi + 1 < n else []
        if b - a == 1:
            sites[gi] = cores[a]
            if nxt and not topo.may_write(cores[a], nxt[0]):
                frelay[gi] = helper(cores[a], [cores[a]], nxt, True)
        else:
            sites[gi] = helper(cores[anchor], [], [cores[r] for r in range(a, b)] + nxt, True)
            for r in range(a, b):
                if not topo.may_write(cores[r], sites[gi]):
                    grelay[r] = helper(cores[r], [cores[r]], [sites[gi]], False)
    a = GROUPS[-1][0]
    srelay = helper(sites[-1], [sites[-1]], cores[a:a + OFFLOAD], True)
    return sites, frelay, grelay, srelay


def _engines(topo, src, dst, n, high):
    m = topo.mask(src, dst)
    bits = [e for e in range(m.bit_length()) if (m >> e) & 1]
    return sum(1 << e for e in (bits[-n:] if high else bits[:n]))


def rank_program(g, core, T, topo):
    sites, frelay, grelay, srelay = _plan(T, topo)
    cores = list(T.cores)
    S = T.sem
    sent = [0]

    def waiter(q):
        seen = {}

        def w(name, val):
            if seen.get(name, 0) < val:
                q.wait_ge(S[name], val)
                seen[name] = val
        return w

    gw, tw, vw, sw, cw = waiter(g), waiter(g.tensor), waiter(g.vector), waiter(g.sync), waiter(g.scalar)

    def send(dst, out_ap, in_ap, rsem, high=False):
        rid, pid = topo.addr(dst, core)
        g.remote_dma(out_ap=out_ap, in_ap=in_ap, remote_sem=S[rsem], local_sem=S.ls, pid=pid, routing_id=rid,
                     dma_engine_mask=_engines(topo, core, dst, ENG, high))
        sent[0] += ENG

    def make_ident(dst):
        g.vector.memset(T.ones[:], 1.0).then_inc(S.fil, 1)
        gw("fil", 1)
        g.affine_select(T.ident[:], T.ones[:], [[-1, 128]], AluOpType.is_equal, 0.0, 0, 1).then_inc(S.sel, 1)
        gw("sel", 1)
        send(dst, T.ident[:], T.ident[:], "idn")

    def col(c0, c1=None):
        return slice(c0 * B, (c0 + 1 if c1 is None else c1) * B)

    def hap(j, c0, c1=None):
        return T.hout[:, j * XW + c0 * B:j * XW + (c0 + 1 if c1 is None else c1) * B]

    def pieces(gi):
        return LAST_PIECES if gi == len(GROUPS) - 1 else [(0, NB)]

    def todo(gi, k):
        return [t[1:] for t in sorted((c1 + j, j, p, c0, c1) for j in range(k) for p, (c0, c1) in enumerate(pieces(gi)))]

    for r, q in grelay.items():
        if q == core:
            gi = [i for i, (a, b, _) in enumerate(GROUPS) if a <= r < b][0]
            j = r - GROUPS[gi][0]
            gw("rs", ENG)
            send(sites[gi], T.gin[:, j * SLOT:(j + 1) * SLOT], T.gin[:, 0:SLOT], "gs%d" % j)
            gw("ls", sent[0])
            return

    for gi, q in enumerate(frelay):
        if q == core:
            if gi == 0:
                make_ident(sites[gi + 1])
            for c in range(NB):
                gw("fw%d" % c, ENG)
                send(sites[gi + 1], T.hin[:, col(c)], T.hin[:, col(c)], "fw%d" % c)
            gw("ls", sent[0])
            return

    if core == srelay:
        for j, p, c0, c1 in todo(len(GROUPS) - 1, OFFLOAD):
            gw("hs%d" % (j * len(LAST_PIECES) + p), ENG)
            send(cores[GROUPS[-1][0] + j], T.yl[:, col(c0, c1)], hap(j, c0, c1), "ys%d" % p)
        gw("ls", sent[0])
        return

    rank = T.rank_of(core)
    if core not in sites:
        if rank is None:
            return
        gi = [i for i, (a, b, _) in enumerate(GROUPS) if a <= rank < b][0]
        j = rank - GROUPS[gi][0]
        g.sync.dma_start(T.gin[:, 0:XW], T.x[:]).then_inc(S.ld, 16)
        g.scalar.dma_start(T.gin[:, XW:XW + WW], T.wv[:]).then_inc(S.ld, 16)
        g.scalar.dma_start(T.gin[:, XW + WW:SLOT], T.wh[:]).then_inc(S.ld, 16)
        gw("ld", 48)
        if rank in grelay:
            send(grelay[rank], T.gin[:, 0:SLOT], T.gin[:, 0:SLOT], "rs")
        else:
            send(sites[gi], T.gin[:, j * SLOT:(j + 1) * SLOT], T.gin[:, 0:SLOT], "gs%d" % j)
        for p, (c0, c1) in enumerate(pieces(gi)):
            sw("ys%d" % p, ENG)
            g.sync.dma_start(T.y[:, col(c0, c1)], T.yl[:, col(c0, c1)]).then_inc(S.st, 16)
        gw("ls", sent[0])
        gw("st", 16 * len(pieces(gi)))
        return

    gi = sites.index(core)
    a, b, _ = GROUPS[gi]
    k = b - a
    own = rank is not None
    first = a == 0
    fdst = None
    if gi + 1 < len(GROUPS):
        fdst = frelay[gi] if frelay[gi] is not None else sites[gi + 1]

    def xap(j, c):
        return T.gin[:, j * SLOT + c * B:j * SLOT + (c + 1) * B]

    def wvap(j):
        return T.gin[:, j * SLOT + XW:j * SLOT + XW + WW]

    def whap(j):
        return T.gin[:, j * SLOT + XW + WW:(j + 1) * SLOT]

    g.vector.memset(T.z32[:], 0.0).then_inc(S.zs, 1)
    nz = 1
    if first:
        g.vector.memset(T.z16[:], 0.0).then_inc(S.zs, 1)
        nz = 2
        g.sync.dma_start(xap(0, 0), T.x[:, col(0)]).then_inc(S.lx0, 16)
        g.scalar.dma_start(whap(0), T.wh[:]).then_inc(S.lw, 16)
        g.sync.dma_start(T.gin[:, B:XW], T.x[:, B:XW]).then_inc(S.lx1, 16)
        if frelay[gi] is None and fdst is not None:
            make_ident(fdst)
    else:
        if fdst is not None:
            gw("idn", ENG)
            send(fdst, T.ident[:], T.ident[:], "idn")
        if own:
            g.scalar.dma_start(T.gin[:, 0:XW], T.x[:]).then_inc(S.gs0, 16)
            g.scalar.dma_start(wvap(0), T.wv[:]).then_inc(S.gs0, 16)
            g.scalar.dma_start(whap(0), T.wh[:]).then_inc(S.gs0, 16)
    vw("zs", nz)

    def got(w, j, what, c=0):
        if first:
            if what == "w":
                w("lw", 16)
            else:
                w("lx0" if c == 0 else "lx1", 16)
        else:
            w("gs%d" % j, 48 if own else ENG)

    seq = [(j, d - j) for d in range(NB + k - 1) for j in reversed(range(k)) if 0 <= d - j < NB]

    def mats(j, c):
        m = []
        if not first:
            m.append((T.ident[:], xap(j, c), ("idn", ENG)))
        if c > 0:
            m.append((whap(j), hap(j, c - 1), ("vd%d" % j, c)))
        if a + j > 0:
            if j > 0:
                m.append((wvap(j), hap(j - 1, c), ("vd%d" % (j - 1), c + 1)))
            else:
                m.append((wvap(j), T.hin[:, col(c)], ("fw%d" % c, ENG)))
        return m

    def issue(i, opening):
        j, c = seq[i]
        m = mats(j, c)
        ps = T["ps%d" % (i % NBANK)][:, 0:B]
        for n_, e in enumerate(m):
            if (not first and n_ == 0) != opening:
                continue
            if n_ == 0 and i >= NBANK:
                pj, pc = seq[i - NBANK]
                tw("vd%d" % pj, pc + 1)
            got(tw, j, "w")
            tw(e[2][0], e[2][1])
            ins = g.tensor.matmul(ps, e[0], e[1], n_ == 0, n_ == len(m) - 1)
            if n_ == len(m) - 1:
                ins.then_inc(S["md%d" % j], 1)

    nva = 0
    issue(0, True)
    for i, (j, c) in enumerate(seq):
        ps = T["ps%d" % (i % NBANK)][:, 0:B]
        if i + 1 < len(seq):
            issue(i + 1, True)
        issue(i, False)
        if mats(j, c):
            vw("md%d" % j, c if first else c + 1)
            if first:
                got(vw, j, "x", c)
                g.vector.tensor_tensor(ps, ps, xap(j, c), AluOpType.add).then_inc(S.va, 1)
                nva += 1
                vw("va", nva)
            g.vector.tensor_tensor(hap(j, c), ps, T.z32[:], AluOpType.max).then_inc(S["vd%d" % j], 1)
        else:
            got(vw, j, "x", c)
            g.vector.tensor_tensor(hap(j, c), xap(j, c), T.z16[:], AluOpType.max).then_inc(S["vd%d" % j], 1)

    nst = 0
    for c in range(NB):
        if fdst is not None:
            gw("vd%d" % (k - 1), c + 1)
            send(fdst, T.hin[:, col(c)], hap(k - 1, c), "fw%d" % c)
        if own and not first:
            q, w = (g.sync, sw) if c % 2 == 0 else (g.scalar, cw)
            w("vd0", c + 1)
            q.dma_start(T.y[:, col(c)], hap(0, c)).then_inc(S.st, 16)
            nst += 1
    if own and first:
        sw("vd0", NB)
        g.sync.dma_start(T.y[:], T.hout[:, 0:XW]).then_inc(S.st, 16)
        nst += 1
    if not own:
        for j, p, c0, c1 in todo(gi, k):
            gw("vd%d" % j, c1)
            if fdst is None and j < OFFLOAD:
                send(srelay, hap(j, c0, c1), hap(j, c0, c1), "hs%d" % (j * len(LAST_PIECES) + p), high=True)
            else:
                send(cores[a + j], T.yl[:, col(c0, c1)], hap(j, c0, c1), "ys%d" % p, high=True)
    for j in range(k):
        gw("vd%d" % j, NB)
    if sent[0]:
        gw("ls", sent[0])
    if nst:
        gw("st", 16 * nst)
